import numpy as np, ml_dtypes
CORES = [10,34,74,98]
N = 4
BF = ml_dtypes.bfloat16
def gentries(a):
    return np.ascontiguousarray(a.reshape(8, 16, -1).transpose(0, 2, 1)).reshape(8, -1)
def gtable(e):
    e = np.asarray(e); return np.ascontiguousarray(e.reshape(8, -1, 16).transpose(0, 2, 1)).reshape(128, -1).astype(np.int32)
V, S, G, OFF, DEP, Q = 4096, 2048, 256, (1, 3), 5, 9
B = len(OFF); W = S + B * G
def parts(rng):
    h = rng.integers(0, 128, (N, 8, 16, V)); v = rng.integers(0, 128, (N, 8, 16, S))
    e = rng.integers(0, 16, (N, 8, V)); k0 = rng.integers(0, V, (N, 8, V)); k1 = rng.integers(0, V, (N, 8, V))
    p = rng.integers(0, W, (N, 8, 16, S)); n = rng.integers(0, V, (N, 8, S))
    b = np.ascontiguousarray(np.argsort(rng.random((N, 8, B, S)), axis=-1)[..., :G])
    return h, v, e, k0, k1, p, n, b
def pack(h, v, e, k0, k1, p, n, b):
    return {"hist": np.ascontiguousarray(h.reshape(N, 128, V)).astype(np.float32).astype(BF), "x": np.ascontiguousarray(v.reshape(N, 128, S)).astype(np.float32).astype(BF),
            "way": e.astype(np.int32), "kid0": k0.astype(np.int32), "kid1": k1.astype(np.int32), "nb": np.ascontiguousarray(p.reshape(N, 128, S)).astype(np.int32),
            "nd0": np.stack([gtable(a) for a in n]), "bd": np.stack([gtable(a.reshape(8, -1)) for a in b])}
def setup_inputs(rng):
    return pack(*parts(rng))
def setup_inputs_ties(rng):
    h, v, e, k0, k1, p, n, b = parts(rng)
    hb = rng.choice(np.array([0, 63, 126]), (1, 8, 16, 1)); xb = rng.choice(np.array([0, 64, 127]), (1, 8, 16, 1))
    hb[0, 0] = 126; xb[0, 0] = 127; hb[0, 1] = 0; xb[0, 1] = 0
    k = rng.choice(np.array([0, 0, 0, 0, Q - 1, Q, Q + 1, 16]), (N, 8, 1, V))
    place = np.argsort(rng.random((N, 8, 16, V)), axis=2)
    h = hb + (place < k); v = np.zeros((N, 8, 16, S), np.int64) + xb
    ends = np.array([0, 1, 126, 127])
    h[:, 6:] = rng.choice(ends, (N, 2, 16, V)); v[:, 6:] = rng.choice(ends, (N, 2, 16, S))
    return pack(h, v, e, k0, k1, p, n, b)
def setup_inputs_alike(rng):
    h, v, e, k0, k1, p, n, b = parts(rng)
    p[:, 1] = np.arange(S); p[:, 2] = rng.integers(S, W, (N, 16, S)); p[:, 3] = rng.integers(0, S, (N, 16, S))
    p[:, 4] = rng.choice(np.array([0, S - 1, S, S + G - 1, W - G, W - 1]), (N, 16, S)); p[:, 5] = rng.integers(0, W, (N, 1, 1)); p[:, 6] = p[:, 6, :1]
    b[:, ::2] = rng.choice(np.array([0, S - 1, S // 2, 3]), (N, 4, B, G))
    e[:, 2:4] = rng.integers(0, 16, (N, 2, 1))
    b[:, 0] = rng.integers(1, S, (N, B, 1)); b[:, 7] = np.argsort(rng.random((N, S)), axis=-1)[:, :B * G].reshape(N, B, G)
    n[:, ::7] = np.argsort(rng.random((N, 2, V)), axis=-1)[..., :S]
    return pack(h, v, e, k0, k1, p, n, b)
def setup_inputs_meet(rng):
    h, v, e, k0, k1, p, n, b = parts(rng)
    n[:, :4] = rng.choice(np.array([0, 1, V // 2, V - 1]), (N, 4, S)); n[:, 0] = 0; n[:, 7] = V - 1 - rng.integers(0, 32, (N, S))
    k1[:, 2] = k0[:, 2]; k0[:, 3] = np.arange(V); k1[:, 3] = np.arange(V); k0[:, 4] = np.arange(V)
    k0[:, 5] = rng.choice(np.array([0, V - 1]), (N, V)); k1[:, 5] = rng.choice(np.array([0, V - 1]), (N, V))
    e[:, 6] = rng.choice(np.array([0, 15]), (N, V))
    return pack(h, v, e, k0, k1, p, n, b)
def setup_inputs_far(rng):
    h, v, e, k0, k1, p, n, b = parts(rng); half = V // 2
    h = rng.integers(0, 97, (N, 8, 1, 1)) + rng.integers(0, 31, h.shape); v = rng.integers(0, 97, (N, 8, 1, 1)) + rng.integers(0, 31, v.shape)
    p = rng.integers(S, W, p.shape); b[..., 0] = 0; b[..., G - 1] = S - 1
    e[:, :4] = rng.integers(0, 16, (N, 4, 1)); p[:, :2] = rng.integers(S, S + G, (N, 2, 16, S))
    n[:, 0] = rng.integers(0, V, (N, 1)); v[:, 0] = rng.integers(0, 128, (N, 16, S))
    h[:, 0] = rng.integers(0, 32, (N, 16, V)); h[1::2, 0] += 96
    v[:, 1] = rng.integers(0, 32, (N, 16, S)); h[::2, 1] = rng.integers(64, 80, (N // 2, 16, V)); k0[::2, 1] = np.arange(V)
    h[1::2, 1] = rng.integers(0, 128, (N // 2, 16, V)); h[1::2, 1, :, :half] = rng.integers(0, 16, (N // 2, 16, half))
    n[1::2, 1] = rng.integers(0, half, (N // 2, S))
    k0[1::2, 1, :half] = rng.integers(half, V, (N // 2, half)); k1[1::2, 1, :half] = rng.integers(half, V, (N // 2, half))
    return pack(h, v, e, k0, k1, p, n, b)
def setup_inputs_spread(rng):
    h, v, e, k0, k1, p, n, b = parts(rng)
    h = np.minimum((np.exp2(7 * rng.random((N, 8, 1, V))) * rng.random(h.shape)).astype(np.int64), 127)
    v = np.minimum((np.exp2(7 * rng.random((N, 8, 1, S))) * rng.random(v.shape)).astype(np.int64), 127)
    n = np.minimum((V * rng.random(n.shape) ** 3).astype(np.int64), V - 1); k1 = np.minimum((V * rng.random(k1.shape) ** 2).astype(np.int64), V - 1)
    p = W - 1 - np.minimum((W * rng.random(p.shape) ** 2).astype(np.int64), W - 1)
    b[:, ::2] = np.argsort(rng.random((N, 4, B, S // 2)), axis=-1)[..., :G] + S // 2 * rng.integers(0, 2, (N, 4, B, 1))
    return pack(h, v, e, k0, k1, p, n, b)
def check_inputs(d):
    bad = []
    for k in ("hist", "x"):
        a = np.asarray(d[k]).astype(np.float32)
        if not np.all((a >= 0) & (a <= 127) & (a == np.floor(a))): bad.append("whole numbers from 0 to 127 in " + k)
    for k, hi in (("way", 15), ("kid0", V - 1), ("kid1", V - 1), ("nb", W - 1), ("nd0", V - 1), ("bd", S - 1)):
        if np.min(d[k]) < 0 or np.max(d[k]) > hi: bad.append("range of " + k)
    return bad
def reference(hist, x, way, kid0, kid1, nb, nd0, bd):
    h = hist.astype(np.float32).astype(np.int32).reshape(N, 8, 16, V); xv = x.astype(np.float32).astype(np.int32).reshape(N, 8, 16, S)
    part = nb.astype(np.int64).reshape(N, 8, 16, S)
    n = np.stack([gentries(a) for a in nd0]).astype(np.int64)
    bl = np.stack([gentries(a) for a in bd]).astype(np.int64).reshape(N, 8, B, G)
    for depth in range(DEP):
        hn = np.stack([np.take_along_axis(h[a], n[a][:, None, :], 2) for a in range(N)])
        new = []
        for a in range(N):
            hw, xw = [hn[a]], [xv[a]]
            for i, d in enumerate(OFF):
                q = (a - d) % N; ix = bl[q, :, i][:, None, :]
                hw.append(np.take_along_axis(hn[q], ix, 2)); xw.append(np.take_along_axis(xv[q], ix, 2))
            hw, xw = np.concatenate(hw, axis=2), np.concatenate(xw, axis=2)
            e = np.take_along_axis(way[a].astype(np.int64), n[a], 1)
            p = np.take_along_axis(part[a], e[:, None, :], 1)
            more = xv[a] + np.take_along_axis(hw, p, 2) > np.take_along_axis(xw, p, 2) + hn[a]
            right = np.add.reduce(more.astype(np.int32), axis=1) >= Q
            new.append(np.where(right, np.take_along_axis(kid1[a], n[a], 1), np.take_along_axis(kid0[a], n[a], 1)))
        n = np.stack(new).astype(np.int64)
    return {"y": n.astype(np.float32)}

from concourse.mybir import AluOpType as ALU, ActivationFunctionType as ACT

V, S, G, OFF, DEP = 4096, 2048, 256, (1, 3), 5
W = S + len(OFF) * G
H = S // 2
HC = H // 16
SHIFT = W // 2
BANK = 512

SCRATCH = {
    "hs": ("sbuf", [128, V], "bfloat16"), "oh": ("sbuf", [128, V], "bfloat16"), "kt": ("sbuf", [128, V], "bfloat16"),
    "xs": ("sbuf", [128, S], "bfloat16"), "nbi": ("sbuf", [128, S], "int32"), "nbh": ("sbuf", [128, S], "float16"),
    "wi": ("sbuf", [128, 512], "int32"), "wv": ("sbuf", [128, 512], "bfloat16"),
    "kc": ("sbuf", [128, 512], "int32"), "dg": ("sbuf", [128, 1024], "bfloat16"),
    "ndi": ("sbuf", [128, 128], "int32"), "bdi": ("sbuf", [128, 32], "int32"),
    "nl": ("sbuf", [128, 128], "uint16"), "pl": ("sbuf", [128, 128], "uint16"), "bl": ("sbuf", [128, 32], "uint16"),
    "mk": ("sbuf", [128, S], "float16"), "bits": ("sbuf", [128, S], "bfloat16"), "kg": ("sbuf", [128, S], "bfloat16"),
    "own": ("sbuf", [128, S], "bfloat16"),
    "sgn": ("sbuf", [128, 256], "float32"), "scn": ("sbuf", [128, 256], "float32"),
    "fs": ("sbuf", [128, 128], "float32"), "ft": ("sbuf", [128, 128], "float32"), "yo": ("sbuf", [128, 128], "float32"),
    "pi": ("sbuf", [128, 1], "int32"), "ci": ("sbuf", [128, 4], "int32"), "cf": ("sbuf", [128, 4], "float32"),
    "cc": ("sbuf", [128, 4], "float32"),
    "tf": ("sbuf", [128, 144], "float32"), "a8": ("sbuf", [128, 128], "float32"), "co": ("sbuf", [128, 128], "float32"),
    "j8": ("sbuf", [128, 8], "float32"), "mj": ("sbuf", [128, 8], "float32"),
    "g2": ("sbuf", [128, 128], "float32"), "bf": ("sbuf", [128, 128], "bfloat16"), "sel": ("sbuf", [128, 1024], "bfloat16"),
    "w1": ("sbuf", [128, 144], "bfloat16"), "wh": ("sbuf", [128, 144], "float16"), "wm": ("sbuf", [128, 144], "bfloat16"),
    "wd": ("sbuf", [128, 144], "bfloat16"), "we": ("sbuf", [128, 144], "bfloat16"),
    "ps": ("psum", [128, 8 * BANK], "float32"),
}
for _d in range(DEP):
    SCRATCH["dd%d" % _d] = ("sbuf", [128, W], "bfloat16")
    SCRATCH["bs%d" % _d] = ("sbuf", [128, len(OFF) * G], "bfloat16")

SEMAPHORES = ["gi0", "gi1", "ktz", "v", "ldW", "ldN", "ldH", "ldX0", "ldX1", "ldK", "ldB0", "ldB1", "ldT", "sq", "sel", "wv", "cst",
              "dg", "oh0", "oh1", "oh2", "oh3", "ohd", "a", "b0", "b1", "p0", "p1", "pc0", "pc1", "c0", "c1", "c2", "cn0", "cn1",
              "sg0", "sg1", "sc", "n0", "n1", "nbd", "k0", "k1", "kp0", "kp1", "bd0", "bd1", "cv0", "cv1", "cp0", "cp1", "sent",
              "fin", "out"] + ["arr%d" % _d for _d in range(DEP)]


def rank_program(g, core, T, topo):
    rank = T.rank_of(core)
    if rank is None:
        return
    N = len(T.cores)
    vec, act, pe, sp = g.vector, g.scalar, g.tensor, g.sync
    queues = {"g": g, "v": vec, "s": act, "t": pe, "y": sp}
    cnt, seen, top = {}, {}, {}

    def inc(ins, name, n=1):
        ins.then_inc(T.sem[name], n)
        cnt[name] = cnt.get(name, 0) + n

    def wait(q, *names):
        for name in names:
            val = cnt[name]
            if seen.get((q, name), 0) < val:
                queues[q].wait_ge(T.sem[name], val)
                seen[(q, name)] = val
                top[name] = max(top.get(name, 0), val)

    ps = T.ps

    inc(sp.dma_start(T.wi[0:64, :], T.way[:]), "ldW", 16)
    inc(act.dma_start(T.wi[64:128, :], T.way[:]), "ldW", 16)
    inc(act.dma_start(T.ndi[:], T.nd0[:]), "ldN", 16)
    inc(act.dma_start(T.bdi[:], T.bd[:]), "ldN", 16)
    inc(sp.dma_start(T.hs[:], T.hist[:]), "ldH", 16)
    inc(act.dma_start(T.xs[:, 0:H], T.x[:, 0:H]), "ldX0", 16)
    inc(sp.dma_start(T.xs[:, H:S], T.x[:, H:S]), "ldX1", 16)
    inc(sp.dma_start(T.kc[:, 0:256], T.kid0[:]), "ldK", 16)
    inc(sp.dma_start(T.kc[:, 256:512], T.kid1[:]), "ldK", 16)
    inc(sp.dma_start(T.nbi[:, 0:H], T.nb[:, 0:H]), "ldB0", 16)
    inc(sp.dma_start(T.nbi[:, H:S], T.nb[:, H:S]), "ldB1", 16)

    fl = {"allow_small_or_imprecise_dtypes": True}
    inc(g.iota(T.pi[:], [[0, 1]], 0, 1), "gi0")
    inc(g.iota(T.j8[:], [[1, 8]], 0, 0, **fl), "gi1")
    inc(g.iota(T.a8[:], [[1, 8], [0, 16]], 0, 0, **fl), "gi1")
    inc(g.iota(T.co[0:64, :], [[0, 8], [2, 16]], 0, 0, **fl), "gi1")
    inc(g.iota(T.tf[:], [[1, 144]], -15, 0, **fl), "gi1")
    inc(g.iota(T.kt[:, V // 2:V], [[0, V // 2]], 0, 0, **fl), "ktz")
    inc(vec.memset(T.co[64:128, :], -1.0), "v")
    inc(vec.memset(T.sgn[:], 0.0), "v")
    inc(vec.memset(T.kt[:, 0:V // 2], 0.0), "ktz")
    wait("v", "gi0")
    inc(vec.tensor_scalar(T.ci[:, 0:1], T.pi[:], 15, None, ALU.bitwise_and), "v")
    inc(vec.tensor_scalar(T.ci[:, 1:2], T.pi[:], 112, None, ALU.bitwise_and), "v")
    inc(vec.tensor_scalar(T.ci[:, 2:3], T.pi[:], 3, 7, ALU.logical_shift_right, ALU.bitwise_and), "v")
    inc(vec.tensor_scalar(T.ci[:, 3:4], T.pi[:], 7, None, ALU.bitwise_and), "v")
    wait("v", "v")
    inc(vec.tensor_copy(T.cf[:], T.ci[:]), "v")
    wait("v", "v", "gi1")
    row, first, grp, blk = T.cf[:, 0:1], T.cf[:, 1:2], T.cf[:, 2:3], T.cf[:, 3:4]
    inc(vec.tensor_scalar(T.g2[:], T.a8[:], grp, None, ALU.is_equal), "v")
    inc(vec.tensor_scalar(T.mj[:], T.j8[:], blk, None, ALU.is_equal), "v")
    inc(vec.tensor_scalar(T.cc[:, 3:4], row, row, -1.0, ALU.mult, ALU.mult), "v")
    inc(vec.tensor_scalar(T.cc[:, 0:1], row, 4.0, None, ALU.is_lt), "v")
    inc(vec.tensor_scalar(T.cc[:, 1:2], row, 2.0, 0.5, ALU.is_ge, ALU.subtract), "v")
    inc(vec.tensor_scalar(T.w1[:], T.tf[:], first, None, ALU.is_equal), "v")
    wait("v", "v")
    inc(vec.tensor_tensor(T.bf[:], T.g2[:], T.co[:], ALU.mult), "v")
    inc(vec.tensor_scalar(T.cc[:, 2:3], T.cc[:, 3:4], 1.0, None, ALU.add), "cst")
    wait("v", "v", "ldW")
    inc(vec.tensor_copy(T.wv[:], T.wi[:]), "wv")
    for j in range(8):
        inc(vec.tensor_scalar(T.sel[:, 128 * j:128 * j + 128], T.bf[:], T.mj[:, j:j + 1], None, ALU.mult), "sel")
    inc(vec.tensor_scalar(T.wh[:], T.tf[:], first, None, ALU.is_equal), "cst")
    inc(vec.tensor_scalar(T.wm[:], T.w1[:], T.cc[:, 0:1], 0.5, ALU.mult, ALU.mult), "cst")
    inc(vec.tensor_scalar(T.wd[:], T.w1[:], T.cc[:, 0:1], T.cc[:, 1:2], ALU.mult, ALU.mult), "cst")
    wait("v", "cst")
    inc(vec.tensor_scalar(T.we[:], T.wd[:], 2.0, None, ALU.mult), "cst")
    wait("v", "ldN")
    inc(vec.tensor_copy(T.nl[:, 0:HC], T.ndi[:, 0:HC]), "n0")
    inc(vec.tensor_copy(T.nl[:, HC:2 * HC], T.ndi[:, HC:2 * HC]), "n1")
    inc(vec.tensor_copy(T.bl[:], T.bdi[:]), "nbd")

    wait("s", "wv")
    inc(act.activation(T.wv[64:128, :], T.wv[64:128, :], ACT.Square), "sq")
    wait("t", "sel", "wv", "sq")
    for j in range(8):
        inc(pe.matmul(ps[:, BANK * j:BANK * (j + 1)], T.sel[:, 128 * j:128 * j + 128], T.wv[:], True, True), "oh%d" % (j // 2))
    wait("s", "cst")

    def onehot(q):
        wait("s", "oh%d" % q)
        inc(act.activation(T.oh[:, 1024 * q:1024 * (q + 1)], ps[:, 1024 * q:1024 * (q + 1)], ACT.Relu, bias=T.cc[:, 2:3]), "ohd")

    def to_list(out, w, src, h, name):
        for i in range(16):
            ins = pe.matmul(out, w[:, 15 - i:143 - i], src[:, H * h + i:H * (h + 1):16], i == 0, i == 15)
        inc(ins, name)

    def to_rows(out, w, src, t0, t1):
        for t in range(t0, t1):
            ins = pe.matmul(out, w[:, 15 - t:143 - t], src[:, 128 * t:128 * (t + 1)], t == 0, t == 15)
        return ins

    def step_a(d, h):
        wait("v", "n%d" % h)
        if d == 0:
            wait("v", "ldH", "ldX%d" % h)
        inc(vec.tensor_tensor(T["dd%d" % d][:, H * h:H * (h + 1)], T.hs[:, 0:V].indirect(T.nl[:, HC * h:HC * (h + 1)]),
                              T.xs[:, H * h:H * (h + 1)], ALU.subtract), "a")

    def step_b(h):
        inc(vec.tensor_tensor(T.mk[:, H * h:H * (h + 1)], T.oh[:, 0:V].indirect(T.nl[:, HC * h:HC * (h + 1)]),
                              T.nbh[:, H * h:H * (h + 1)], ALU.mult), "b%d" % h)

    def step_k(h, c0, c1):
        wait("s", "n%d" % h)
        inc(act.activation(T.kg[:, 16 * c0:16 * c1], T.kt[:, 0:V].indirect(T.nl[:, c0:c1]), ACT.Copy), "k%d" % h)

    def border(d):
        wait("s", "a", "nbd")
        for b, off in enumerate(OFF):
            inc(act.activation(T["bs%d" % d][:, G * b:G * (b + 1)], T["dd%d" % d][:, 0:S].indirect(T.bl[:, 16 * b:16 * (b + 1)]),
                               ACT.Copy), "bd%d" % b)
            dst = T.cores[(rank + off) % N]
            assert topo.may_write(core, dst)
            rid, pid = topo.addr(dst)[:2]
            wait("g", "bd%d" % b)
            g.remote_dma(T["dd%d" % d][:, S + G * b:S + G * (b + 1)], T["bs%d" % d][:, G * b:G * (b + 1)],
                         T.sem["arr%d" % d], T.sem.sent, pid, rid, topo.mask(core, dst))
            cnt["sent"] = cnt.get("sent", 0) + len(topo.engines(core, dst))
            src = T.cores[(rank - off) % N]
            cnt["arr%d" % d] = cnt.get("arr%d" % d, 0) + len(topo.engines(src, core))

    def own_copy(d):
        for h in range(2):
            inc(act.activation(T.own[:, H * h:H * (h + 1)], T["dd%d" % d][:, H * h:H * (h + 1)], ACT.Copy), "cp%d" % h)

    def kids(d, h):
        wait("t", "k%d" % h)
        if d < DEP - 1:
            to_list(ps[:, BANK * h:BANK * h + 128:2], T.wd, T.kg, h, "kp%d" % h)
            to_list(ps[:, BANK * h + 1:BANK * h + 128:2], T.wm, T.kg, h, "kp%d" % h)
        else:
            i1 = to_rows(ps[:, BANK * 6:BANK * 6 + 128], T.we, T.kg, 8 * h, 8 * h + 8)
            i2 = to_rows(ps[:, BANK * 7:BANK * 7 + 128], T.wm, T.kg, 8 * h, 8 * h + 8)
            if h == 1:
                inc(i1, "kp1")
                inc(i2, "kp1")

    def partners(h):
        wait("t", "b%d" % h)
        to_list(ps[:, BANK * (2 + h):BANK * (2 + h) + HC], T.wh, T.mk, h, "p%d" % h)

    def plist(h):
        wait("v", "p%d" % h)
        inc(vec.tensor_scalar(T.pl[:, HC * h:HC * (h + 1)], ps[:, BANK * (2 + h):BANK * (2 + h) + HC], float(SHIFT), None, ALU.add),
            "pc%d" % h)
        wait("v", "pc%d" % h, "cp%d" % h)

    def step_c(d, s0, s1, name):
        wait("v", "a", "arr%d" % d)
        inc(vec.tensor_tensor(T.bits[:, s0:s1], T["dd%d" % d][:, 0:W].indirect(T.pl[:, s0 // 16:s1 // 16]),
                              T.own[:, s0:s1], ALU.is_gt), name)

    def sign(h):
        wait("s", "cn%d" % h)
        inc(act.activation(T.sgn[:, 128 * h + 1:128 * (h + 1):2], ps[:, BANK * (4 + h):BANK * (4 + h) + HC], ACT.Sign, bias=-8.5),
            "sg%d" % h)

    def choose(h):
        wait("v", "sg%d" % h, "kp%d" % h)
        inc(vec.tensor_tensor_scan(T.scn[:, 128 * h:128 * (h + 1)], T.sgn[:, 128 * h:128 * (h + 1)], ps[:, BANK * h:BANK * h + 128],
                                   0.0, ALU.mult, ALU.add), "sc")
        wait("v", "sc")
        inc(vec.tensor_copy(T.nl[:, HC * h:HC * (h + 1)], T.scn[:, 128 * h + 1:128 * (h + 1):2]), "n%d" % h)

    for q in range(3):
        onehot(q)
    step_a(0, 0)
    step_a(0, 1)
    border(0)
    onehot(3)
    own_copy(0)
    wait("t", "ohd", "cst", "v")
    wait("v", "ldK")
    inc(vec.tensor_copy(T.dg[:, 0:512], T.kc[:]), "v")
    wait("v", "v")
    inc(vec.tensor_tensor(T.dg[:, 512:1024], T.kc[:], T.dg[:, 0:512], ALU.subtract), "dg")
    wait("y", "dg", "ktz")
    for r, c0 in enumerate((0, 512, 256, 768)):
        inc(sp.dma_start(T.kt[r:128:16, :], T.dg[:, c0:c0 + 256]), "ldT", 16)
    for h in range(2):
        wait("v", "ldB%d" % h)
        inc(vec.tensor_scalar(T.nbh[:, H * h:H * (h + 1)], T.nbi[:, H * h:H * (h + 1)], float(-SHIFT), None, ALU.add), "cv%d" % h)
        wait("v", "cv%d" % h, "ohd")
        step_b(h)
        partners(h)
    wait("s", "ldT")
    for h in range(2):
        step_k(h, HC * h, HC * (h + 1))
        kids(0, h)

    for d in range(DEP - 1):
        for h in range(2):
            plist(h)
            step_c(d, H * h, H * (h + 1), "c%d" % h)
            wait("t", "c%d" % h)
            to_list(ps[:, BANK * (4 + h):BANK * (4 + h) + HC], T.w1, T.bits, h, "cn%d" % h)
        sign(0)
        choose(0)
        step_k(0, 0, HC // 2)
        sign(1)
        step_k(0, HC // 2, HC)
        step_a(d + 1, 0)
        choose(1)
        step_k(1, HC, 2 * HC)
        step_a(d + 1, 1)
        border(d + 1)
        own_copy(d + 1)
        kids(d + 1, 0)
        kids(d + 1, 1)
        for h in range(2):
            step_b(h)
            partners(h)

    d = DEP - 1
    cps = ps[:, BANK * 4:BANK * 4 + 128]
    for k, (t0, t1) in enumerate(((0, 8), (8, 14), (14, 16))):
        if k < 2:
            plist(k)
        step_c(d, 128 * t0, 128 * t1, "c%d" % k)
        wait("t", "c%d" % k)
        ins = to_rows(cps, T.w1, T.bits, t0, t1)
    inc(ins, "cn0")
    wait("v", "cn0", "kp1")
    inc(vec.tensor_scalar(T.fs[:], cps, 8.5, 0.5, ALU.is_ge, ALU.subtract), "v")
    wait("v", "v")
    inc(vec.tensor_tensor(T.ft[:], T.fs[:], ps[:, BANK * 6:BANK * 6 + 128], ALU.mult), "v")
    wait("v", "v")
    inc(vec.tensor_tensor(T.yo[:], T.ft[:], ps[:, BANK * 7:BANK * 7 + 128], ALU.add), "fin")
    wait("y", "fin")
    inc(sp.dma_start(T.y[:], T.yo[:]), "out", 16)
    wait("y", "out")
    for name in sorted(cnt):
        if top.get(name, 0) < cnt[name]:
            wait("g", name)
